import numpy as np
import ml_dtypes


def mxq(x, axis, fmt="e4m3"):
    dtype, down = {"e4m3": (ml_dtypes.float8_e4m3fn, 7), "e5m2": (ml_dtypes.float8_e5m2, 14)}[fmt]
    v = np.moveaxis(np.asarray(x, np.float32).astype(ml_dtypes.bfloat16).astype(np.float64), axis, -1)
    blocks = v.reshape(v.shape[:-1] + (-1, 32))
    amax = np.abs(blocks).max(-1, keepdims=True)
    byte = np.maximum(np.where(amax > 0, np.frexp(amax)[1] - 1 + 127, 0) - down, 1)
    scale = np.exp2(byte - 127.0)
    codes = (blocks / scale).astype(np.float32).astype(dtype).astype(np.float64)
    return np.moveaxis((codes * scale).reshape(v.shape), -1, axis)


WIDE = False


def mx_kscale(k):
    if not WIDE:
        return np.ones(k)
    levels = np.array([10, -10, 5, -5, 0])
    if k % 512:
        return np.exp2(np.random.permutation(np.resize(levels, k // 32))).repeat(32)
    a = np.empty((k // 512, 16))
    for p in range(k // 512):
        a[p, :8] = np.random.permutation(np.resize(levels, 8))
        for g in range(8):
            far = levels[np.abs(levels - a[p, g]) >= 10]
            a[p, g + 8] = far[np.random.randint(len(far))]
    return np.exp2(a.ravel()).repeat(32)


def f64(x):
    return np.asarray(x).astype(np.float64)


def striped(idx):
    return np.tile(np.asarray(idx).reshape(-1, 16).T, (8, 1)).astype(np.uint16)


def unstriped(offs):
    return offs[:16].T.reshape(-1).astype(np.int64)


E2M1 = np.array([0.0, 0.5, 1.0, 1.5, 2.0, 3.0, 4.0, 6.0, -0.0, -0.5, -1.0, -1.5, -2.0, -3.0, -4.0, -6.0])


def pack_weight(w, fmt):
    k, n = w.shape
    w = f64(np.asarray(w, np.float32).astype(ml_dtypes.bfloat16)).reshape(k // 32, 32, n)
    amax = np.abs(w).max(1)
    if fmt == "e4m3":
        byte = np.frexp(amax)[1] - 1 + 127 - 7
    else:
        mant, ex = np.frexp(amax / 6.0)
        byte = np.where(mant > 0.5, ex, ex - 1) + 127
    byte = np.clip(np.where(amax > 0, byte, 1), 1, 254)
    scaled = (w * np.exp2(127.0 - byte)[:, None, :]).reshape(k, n).astype(np.float32)
    by_word = np.ascontiguousarray(scaled.reshape(k // 512, 128, 4, n).transpose(0, 1, 3, 2))
    if fmt == "e4m3":
        words = by_word.astype(ml_dtypes.float8_e4m3fn).view(np.uint8)
    else:
        c = by_word.astype(ml_dtypes.float4_e2m1fn).view(np.uint8) & 0xF
        words = (c[..., 0::2] | (c[..., 1::2] << 4)).reshape(k // 512, 128, 2 * n)
    return np.ascontiguousarray(words), np.ascontiguousarray(byte.astype(np.uint8).reshape(k // 512, 16, n))


def unpack_weight(words, scales, fmt):
    g, _, n = scales.shape
    words = np.ascontiguousarray(words).reshape(g, 128, n, -1)
    if fmt == "e4m3":
        vals = words.view(ml_dtypes.float8_e4m3fn).astype(np.float64)
    else:
        nib = np.empty((g, 128, n, 4), np.uint8)
        nib[..., 0::2] = words & 0xF
        nib[..., 1::2] = words >> 4
        vals = E2M1[nib]
    vals = vals * np.repeat(np.exp2(scales.astype(np.float64) - 127.0), 8, axis=1)[..., None]
    return vals.transpose(0, 1, 3, 2).reshape(g * 512, n)


D, V, I, Q, T = 512, 2048, 512, 128, 4096


def setup_inputs():
    n = np.random.standard_normal
    idx = np.random.permutation(T)[:V]
    idx2 = np.random.randint(0, V, I)
    fd = mx_kscale(D)
    vocp = pack_weight(n((D, T)) / fd[:, None], "e4m3")
    return {
        "hid": (n((D, Q)) * 1.0 / np.sqrt(D) * fd[:, None]).astype(np.float32),
        "voc_words": vocp[0],
        "voc_scales": vocp[1],
        "old": (np.random.uniform(0.0, 1.0, (Q, I))).astype(np.float32),
        "skip": (np.random.uniform(0.0, 1.0, (1, I))).astype(np.float32),
        "offs": striped(idx),
        "offs2": striped(idx2),
    }


def reference(hid, voc_words, voc_scales, old, skip, offs, offs2):
    idx = unstriped(offs)
    idx2 = unstriped(offs2)
    vocu = unpack_weight(voc_words, voc_scales, "e4m3")
    hidq = mxq(f64(hid), 0, "e4m3")
    vocidxg = vocu[:, idx]
    a = hidq.T @ vocidxg
    p = np.exp(a - np.max(a, axis=1, keepdims=True))
    w = p / np.sum(p, axis=1, keepdims=True) * 2048.0
    b1 = np.pad(f64(old), ((0, 0), (1, 0)))[:, :I]
    b2 = np.pad(f64(old), ((0, 0), (2, 0)))[:, :I]
    y = (f64(old) + b1 + b2 * f64(skip)) * w[:, idx2]
    return y

@@ -1,0 +1,183 @@
+from contextlib import ExitStack
+
+import concourse.mybir as mybir
+
+D, V, I, Q, T = 512, 2048, 512, 128, 4096
+FLOPS = 2 * D * V * Q
+
+F32 = mybir.dt.float32
+BF16 = mybir.dt.bfloat16
+I32 = mybir.dt.int32
+U32 = mybir.dt.uint32
+U16 = mybir.dt.uint16
+U8 = mybir.dt.uint8
+FP8X4 = mybir.dt.float8_e4m3fn_x4
+ALU = mybir.AluOpType
+ACT = mybir.ActivationFunctionType
+
+P = 128
+PACK = 4
+LANES = 16
+PAD = 8
+CHUNKS = (512, 512, 512, 256, 256)
+HALF = I // 2
+
+
+def tile_attend_labelforward_kernel(tc, hid, voc_words, voc_scales, old, skip, offs, offs2, out):
+    nc = tc.nc
+    n_chunks = len(CHUNKS)
+    starts = [sum(CHUNKS[:c]) for c in range(n_chunks)]
+
+    with ExitStack() as ctx:
+        keep = ctx.enter_context(tc.tile_pool(name="keep", bufs=1))
+        shared = ctx.enter_context(tc.tile_pool(name="shared", bufs=1))
+        psum = ctx.enter_context(tc.psum_pool(name="psum", bufs=1))
+
+        idx = keep.tile([P, V // LANES], U16, name="idx")
+        idx2 = keep.tile([P, I // LANES], U16, name="idx2")
+        store_scales = shared.tile([P, T], U8, name="store_scales", align_bytes=64, offset=0)
+        zeros = keep.tile([P, P], F32, name="zeros", tag="store", align_bytes=64)
+        hid_raw = keep.tile([P, PACK, Q], F32, name="hid_raw")
+        old_pad = keep.tile([P, PAD + I], F32, name="old_pad")
+        skip_col = keep.tile([P, I // P], F32, name="skip_col")
+        ident = keep.tile([P, P], F32, name="ident")
+
+        nc.vector.memset(store_scales[:].bitcast(I32), 0)
+        nc.sync.dma_start(idx[:], offs)
+        for r in range(PACK):
+            nc.scalar.dma_start(
+                out=store_scales[r:P:32, :].bitcast(I32),
+                in_=voc_scales[0, r:16:PACK, :].bitcast(I32),
+            )
+        nc.sync.dma_start(out=hid_raw[:], in_=hid.rearrange("(p j) q -> p j q", j=PACK))
+        nc.vector.memset(zeros[:], 0.0)
+        nc.gpsimd.affine_select(
+            out=ident[:], in_=zeros[:], compare_op=ALU.not_equal, fill=1.0,
+            base=0, pattern=[[-1, P]], channel_multiplier=1,
+        )
+        store_words = keep.tile([P, T], U32, name="store_words", tag="store", align_bytes=64)
+        nc.sync.dma_start(
+            out=store_words[:].bitcast(I32),
+            in_=voc_words[0].rearrange("p n t -> p (n t)").bitcast(I32),
+            max_dma_last_dim=4096,
+        )
+        nc.sync.dma_start(idx2[:], offs2)
+
+        hid_bf = keep.tile([P, Q, PACK], BF16, name="hid_bf", align_bytes=64)
+        hid_codes = keep.tile([P, Q], U32, name="hid_codes", align_bytes=64)
+        hid_scales = keep.tile([P, Q], U8, name="hid_scales", align_bytes=64)
+        nc.vector.tensor_copy(out=hid_bf[:], in_=hid_raw[:].rearrange("p j q -> p q j"))
+        nc.vector.quantize_mx(
+            out=hid_codes[:].bitcast(FP8X4),
+            scales=hid_scales[:],
+            in_=hid_bf[:].rearrange("p q j -> p (q j)"),
+        )
+
+        nc.gpsimd.memset(old_pad[:, PAD - 4 : PAD], 0.0)
+        nc.gpsimd.dma_start(out=old_pad[:, PAD:], in_=old)
+        with nc.allow_non_contiguous_dma(reason="one value of skip to a partition"):
+            nc.scalar.dma_start(out=skip_col[:], in_=skip[0].rearrange("(j p) -> p j", p=P))
+
+        near_t = psum.tile([P, I], F32, name="near_t")
+        far_t = psum.tile([P, I], F32, name="far_t")
+        coef_ps = psum.tile([P, I], F32, name="coef_ps")
+        near_sb = keep.tile([P, I], F32, name="near_sb")
+        far_sb = keep.tile([P, I], F32, name="far_sb")
+        coef = keep.tile([P, I], F32, name="coef")
+        for j in range(I // P):
+            cols = slice(j * P, (j + 1) * P)
+            for back in (0, 1):
+                first = PAD + j * P - back
+                nc.tensor.matmul(
+                    near_t[:, cols], lhsT=old_pad[:, first : first + P], rhs=ident[:],
+                    is_transpose=True, start=(back == 0), stop=(back == 1),
+                )
+        for j in range(I // P):
+            first = PAD + j * P - 2
+            nc.tensor.transpose(far_t[:, j * P : (j + 1) * P], old_pad[:, first : first + P], ident[:])
+        nc.scalar.copy(out=near_sb[:], in_=near_t[:])
+        for j in range(I // P):
+            cols = slice(j * P, (j + 1) * P)
+            nc.scalar.activation(out=far_sb[:, cols], in_=far_t[:, cols], func=ACT.Copy, scale=skip_col[:, j : j + 1])
+        for j in range(I // P):
+            cols = slice(j * P, (j + 1) * P)
+            for k, part in enumerate((near_sb, far_sb)):
+                nc.tensor.matmul(
+                    coef_ps[:, cols], lhsT=part[:, cols], rhs=ident[:],
+                    is_transpose=True, start=(k == 0), stop=(k == 1),
+                )
+        nc.scalar.copy(out=coef[:], in_=coef_ps[:])
+
+        voc_sc = keep.tile([P, V], U8, name="voc_sc", align_bytes=64)
+        nc.vector.tensor_copy(voc_sc[:], store_scales[:].indirect(idx[:]))
+
+        neg_a = keep.tile([P, V], F32, name="neg_a")
+        p_un = keep.tile([P, V], F32, name="p_un")
+        neg_max = keep.tile([P, 8], F32, name="neg_max")
+        sums = keep.tile([P, 8], F32, name="sums")
+        fix = keep.tile([P, 8], F32, name="fix")
+        for c in range(n_chunks):
+            n = CHUNKS[c]
+            cols = slice(starts[c], starts[c] + n)
+            words = shared.tile([P, n], U32, name="words", align_bytes=64, offset=0, bufs=2)
+            nc.vector.tensor_copy(
+                words[:], store_words[:].indirect(idx[:, starts[c] // LANES : (starts[c] + n) // LANES])
+            )
+            scores = psum.tile([P, n], F32, name="scores%d" % c)
+            nc.tensor.matmul_mx(
+                out=scores[:],
+                lhsT=hid_codes[:].bitcast(FP8X4),
+                lhsT_scale=hid_scales[:],
+                rhs=words[:].bitcast(FP8X4),
+                rhs_scale=voc_sc[:, cols],
+                start=True,
+                stop=True,
+            )
+            nc.vector.tensor_scalar(
+                out=neg_a[:, cols],
+                in0=scores[:],
+                scalar1=-1.0,
+                scalar2=(neg_max[:, c - 1 : c] if c > 0 else None),
+                op0=ALU.mult,
+                op1=ALU.min,
+                accum_out=neg_max[:, c : c + 1],
+            )
+            if c == n_chunks - 1:
+                nc.scalar.activation(
+                    out=fix[:, :n_chunks], in_=neg_max[:, :n_chunks], func=ACT.Exp,
+                    scale=-1.0, bias=neg_max[:, c : c + 1],
+                )
+            nc.scalar.activation(
+                out=p_un[:, cols], in_=neg_a[:, cols], func=ACT.Exp,
+                scale=-1.0, bias=neg_max[:, c : c + 1], accum_out=sums[:, c : c + 1],
+            )
+
+        parts = keep.tile([P, 8], F32, name="parts")
+        total = keep.tile([P, 1], F32, name="total")
+        inv = keep.tile([P, 1], F32, name="inv")
+        gain = keep.tile([P, 8], F32, name="gain")
+        nc.vector.scalar_tensor_tensor(
+            out=parts[:, :n_chunks], in0=sums[:, :n_chunks], scalar=1.0 / V, in1=fix[:, :n_chunks],
+            op0=ALU.mult, op1=ALU.mult, accum_out=total[:],
+        )
+        nc.vector.reciprocal(out=inv[:], in_=total[:])
+        w = keep.tile([P, V], F32, name="w")
+        nc.scalar.activation(out=gain[:, :n_chunks], in_=fix[:, :n_chunks], func=ACT.Copy, scale=inv[:])
+        for c in range(n_chunks):
+            cols = slice(starts[c], starts[c] + CHUNKS[c])
+            if c < 3:
+                nc.vector.tensor_scalar(
+                    out=w[:, cols], in0=p_un[:, cols], scalar1=fix[:, c : c + 1], scalar2=inv[:],
+                    op0=ALU.mult, op1=ALU.mult,
+                )
+            else:
+                nc.scalar.activation(out=w[:, cols], in_=p_un[:, cols], func=ACT.Copy, scale=gain[:, c : c + 1])
+
+        res_a = keep.tile([P, HALF], F32, name="res_a")
+        picked = keep.tile([P, HALF], F32, name="picked")
+        res_b = keep.tile([P, HALF], F32, name="res_b")
+        nc.vector.tensor_tensor(res_a[:], w[:].indirect(idx2[:, : HALF // LANES]), coef[:, :HALF], ALU.mult)
+        nc.scalar.activation(picked[:], w[:].indirect(idx2[:, HALF // LANES :]), ACT.Copy)
+        nc.sync.dma_start(out=out[:, :HALF], in_=res_a[:])
+        nc.vector.tensor_tensor(res_b[:], picked[:], coef[:, HALF:], ALU.mult)
+        nc.sync.dma_start(out=out[:, HALF:], in_=res_b[:])

@@ -1,6 +1,7 @@
 from contextlib import ExitStack
 
 import concourse.mybir as mybir
+from concourse.masks import make_identity
 
 D, V, I, Q, T = 512, 2048, 512, 128, 4096
 FLOPS = 2 * D * V * Q
@@ -36,7 +37,7 @@ def tile_attend_labelforward_kernel(tc, hid, voc_words, voc_scales, old, skip, o
         idx = keep.tile([P, V // LANES], U16, name="idx")
         idx2 = keep.tile([P, I // LANES], U16, name="idx2")
         store_scales = shared.tile([P, T], U8, name="store_scales", align_bytes=64, offset=0)
-        zeros = keep.tile([P, P], F32, name="zeros", tag="store", align_bytes=64)
+        zeros = keep.tile([P, PAD], F32, name="zeros", tag="store", align_bytes=64)
         hid_raw = keep.tile([P, PACK, Q], F32, name="hid_raw")
         old_pad = keep.tile([P, PAD + I], F32, name="old_pad")
         skip_col = keep.tile([P, I // P], F32, name="skip_col")
@@ -44,39 +45,27 @@ def tile_attend_labelforward_kernel(tc, hid, voc_words, voc_scales, old, skip, o
 
         nc.vector.memset(store_scales[:].bitcast(I32), 0)
         nc.sync.dma_start(idx[:], offs)
+        nc.sync.dma_start(out=old_pad[:, PAD:], in_=old)
+        nc.sync.dma_start(out=hid_raw[:], in_=hid.rearrange("(p j) q -> p j q", j=PACK))
+        with nc.allow_non_contiguous_dma(reason="one value of skip to a partition"):
+            nc.gpsimd.dma_start(out=skip_col[:], in_=skip[0].rearrange("(j p) -> p j", p=P))
+        nc.sync.dma_start(idx2[:], offs2)
         for r in range(PACK):
-            nc.scalar.dma_start(
+            nc.sync.dma_start(
                 out=store_scales[r:P:32, :].bitcast(I32),
                 in_=voc_scales[0, r:16:PACK, :].bitcast(I32),
             )
-        nc.sync.dma_start(out=hid_raw[:], in_=hid.rearrange("(p j) q -> p j q", j=PACK))
         nc.vector.memset(zeros[:], 0.0)
-        nc.gpsimd.affine_select(
-            out=ident[:], in_=zeros[:], compare_op=ALU.not_equal, fill=1.0,
-            base=0, pattern=[[-1, P]], channel_multiplier=1,
-        )
+        nc.vector.tensor_copy(out=old_pad[:, :PAD], in_=zeros[:])
+        make_identity(nc, ident[:])
         store_words = keep.tile([P, T], U32, name="store_words", tag="store", align_bytes=64)
         nc.sync.dma_start(
             out=store_words[:].bitcast(I32),
             in_=voc_words[0].rearrange("p n t -> p (n t)").bitcast(I32),
-            max_dma_last_dim=4096,
         )
-        nc.sync.dma_start(idx2[:], offs2)
 
         hid_bf = keep.tile([P, Q, PACK], BF16, name="hid_bf", align_bytes=64)
-        hid_codes = keep.tile([P, Q], U32, name="hid_codes", align_bytes=64)
-        hid_scales = keep.tile([P, Q], U8, name="hid_scales", align_bytes=64)
-        nc.vector.tensor_copy(out=hid_bf[:], in_=hid_raw[:].rearrange("p j q -> p q j"))
-        nc.vector.quantize_mx(
-            out=hid_codes[:].bitcast(FP8X4),
-            scales=hid_scales[:],
-            in_=hid_bf[:].rearrange("p q j -> p (q j)"),
-        )
-
-        nc.gpsimd.memset(old_pad[:, PAD - 4 : PAD], 0.0)
-        nc.gpsimd.dma_start(out=old_pad[:, PAD:], in_=old)
-        with nc.allow_non_contiguous_dma(reason="one value of skip to a partition"):
-            nc.scalar.dma_start(out=skip_col[:], in_=skip[0].rearrange("(j p) -> p j", p=P))
+        nc.scalar.copy(out=hid_bf[:], in_=hid_raw[:].rearrange("p j q -> p q j"))
 
         near_t = psum.tile([P, I], F32, name="near_t")
         far_t = psum.tile([P, I], F32, name="far_t")
@@ -111,15 +100,26 @@ def tile_attend_labelforward_kernel(tc, hid, voc_words, voc_scales, old, skip, o
         voc_sc = keep.tile([P, V], U8, name="voc_sc", align_bytes=64)
         nc.vector.tensor_copy(voc_sc[:], store_scales[:].indirect(idx[:]))
 
-        neg_a = keep.tile([P, V], F32, name="neg_a")
-        p_un = keep.tile([P, V], F32, name="p_un")
-        neg_max = keep.tile([P, 8], F32, name="neg_max")
+        hid_codes = shared.tile([P, Q], U32, name="hid_codes", align_bytes=64, offset=0)
+        hid_scales = keep.tile([P, Q], U8, name="hid_scales", align_bytes=64)
+        nc.vector.quantize_mx(
+            out=hid_codes[:].bitcast(FP8X4),
+            scales=hid_scales[:],
+            in_=hid_bf[:].rearrange("p q j -> p (q j)"),
+        )
+
+        last = n_chunks - 1
+        neg_a = keep.tile([P, V + 8], F32, name="neg_a")
+        p_un = keep.tile([P, V + 8], F32, name="p_un")
+        neg_max = neg_a[:, V:]
+        fix = p_un[:, V:]
         sums = keep.tile([P, 8], F32, name="sums")
-        fix = keep.tile([P, 8], F32, name="fix")
+        terms = keep.tile([P, 8], F32, name="terms")
+        nc.gpsimd.memset(fix[:, last : last + 1], 1.0)
         for c in range(n_chunks):
             n = CHUNKS[c]
             cols = slice(starts[c], starts[c] + n)
-            words = shared.tile([P, n], U32, name="words", align_bytes=64, offset=0, bufs=2)
+            words = shared.tile([P, n], U32, name="words", align_bytes=64, offset=Q * 4, bufs=2)
             nc.vector.tensor_copy(
                 words[:], store_words[:].indirect(idx[:, starts[c] // LANES : (starts[c] + n) // LANES])
             )
@@ -142,22 +142,25 @@ def tile_attend_labelforward_kernel(tc, hid, voc_words, voc_scales, old, skip, o
                 op1=ALU.min,
                 accum_out=neg_max[:, c : c + 1],
             )
-            if c == n_chunks - 1:
+            if c < last:
                 nc.scalar.activation(
-                    out=fix[:, :n_chunks], in_=neg_max[:, :n_chunks], func=ACT.Exp,
-                    scale=-1.0, bias=neg_max[:, c : c + 1],
+                    out=p_un[:, cols], in_=neg_a[:, cols], func=ACT.Exp,
+                    scale=-1.0, bias=neg_max[:, c : c + 1], accum_out=sums[:, c : c + 1],
                 )
-            nc.scalar.activation(
-                out=p_un[:, cols], in_=neg_a[:, cols], func=ACT.Exp,
-                scale=-1.0, bias=neg_max[:, c : c + 1], accum_out=sums[:, c : c + 1],
-            )
+        nc.vector.tensor_scalar(
+            out=terms[:, :last], in0=sums[:, :last], scalar1=-1.0, scalar2=None, op0=ALU.add
+        )
+        nc.scalar.activation(
+            out=p_un[:, starts[last] : V + last], in_=neg_a[:, starts[last] : V + last], func=ACT.Exp,
+            scale=-1.0, bias=neg_max[:, last : last + 1], accum_out=terms[:, last : last + 1],
+        )
 
         parts = keep.tile([P, 8], F32, name="parts")
         total = keep.tile([P, 1], F32, name="total")
         inv = keep.tile([P, 1], F32, name="inv")
         gain = keep.tile([P, 8], F32, name="gain")
         nc.vector.scalar_tensor_tensor(
-            out=parts[:, :n_chunks], in0=sums[:, :n_chunks], scalar=1.0 / V, in1=fix[:, :n_chunks],
+            out=parts[:, :n_chunks], in0=terms[:, :n_chunks], scalar=1.0 / V, in1=fix[:, :n_chunks],
             op0=ALU.mult, op1=ALU.mult, accum_out=total[:],
         )
         nc.vector.reciprocal(out=inv[:], in_=total[:])

@@ -22,6 +22,7 @@ LANES = 16
 PAD = 8
 CHUNKS = (512, 512, 512, 256, 256)
 HALF = I // 2
+CAST_SPLIT = 80
 
 
 def tile_attend_labelforward_kernel(tc, hid, voc_words, voc_scales, old, skip, offs, offs2, out):
@@ -32,40 +33,54 @@ def tile_attend_labelforward_kernel(tc, hid, voc_words, voc_scales, old, skip, o
     with ExitStack() as ctx:
         keep = ctx.enter_context(tc.tile_pool(name="keep", bufs=1))
         shared = ctx.enter_context(tc.tile_pool(name="shared", bufs=1))
+        late = ctx.enter_context(tc.tile_pool(name="late", bufs=1))
         psum = ctx.enter_context(tc.psum_pool(name="psum", bufs=1))
 
         idx = keep.tile([P, V // LANES], U16, name="idx")
         idx2 = keep.tile([P, I // LANES], U16, name="idx2")
         store_scales = shared.tile([P, T], U8, name="store_scales", align_bytes=64, offset=0)
-        zeros = keep.tile([P, PAD], F32, name="zeros", tag="store", align_bytes=64)
+        one = late.tile([P, 32], F32, name="one", align_bytes=64, offset=T * 4 - 64)
+        p_un = keep.tile([P, V + 8], F32, name="p_un")
         hid_raw = keep.tile([P, PACK, Q], F32, name="hid_raw")
-        old_pad = keep.tile([P, PAD + I], F32, name="old_pad")
         skip_col = keep.tile([P, I // P], F32, name="skip_col")
         ident = keep.tile([P, P], F32, name="ident")
 
         nc.vector.memset(store_scales[:].bitcast(I32), 0)
         nc.sync.dma_start(idx[:], offs)
-        nc.sync.dma_start(out=old_pad[:, PAD:], in_=old)
         nc.sync.dma_start(out=hid_raw[:], in_=hid.rearrange("(p j) q -> p j q", j=PACK))
         with nc.allow_non_contiguous_dma(reason="one value of skip to a partition"):
-            nc.gpsimd.dma_start(out=skip_col[:], in_=skip[0].rearrange("(j p) -> p j", p=P))
+            nc.scalar.dma_start(out=skip_col[:], in_=skip[0].rearrange("(j p) -> p j", p=P))
         nc.sync.dma_start(idx2[:], offs2)
         for r in range(PACK):
             nc.sync.dma_start(
                 out=store_scales[r:P:32, :].bitcast(I32),
                 in_=voc_scales[0, r:16:PACK, :].bitcast(I32),
             )
-        nc.vector.memset(zeros[:], 0.0)
-        nc.vector.tensor_copy(out=old_pad[:, :PAD], in_=zeros[:])
-        make_identity(nc, ident[:])
-        store_words = keep.tile([P, T], U32, name="store_words", tag="store", align_bytes=64)
+        nc.vector.memset(one[:, :1], 1.0)
+        nc.vector.tensor_copy(out=p_un[:, V + n_chunks - 1 : V + n_chunks], in_=one[:, :1])
+        nc.vector.memset(ident[:], 0.0)
+        make_identity(nc, ident[:], nomemset=True)
+        old_pad = late.tile([P, PAD + I], F32, name="old_pad", align_bytes=64, offset=T * 4)
+        store_words = late.tile([P, T], U32, name="store_words", align_bytes=64, offset=0)
+        nc.sync.dma_start(out=old_pad[:, PAD:], in_=old)
+        nc.gpsimd.memset(old_pad[:, PAD - 4 : PAD], 0.0)
         nc.sync.dma_start(
             out=store_words[:].bitcast(I32),
             in_=voc_words[0].rearrange("p n t -> p (n t)").bitcast(I32),
         )
 
         hid_bf = keep.tile([P, Q, PACK], BF16, name="hid_bf", align_bytes=64)
-        nc.scalar.copy(out=hid_bf[:], in_=hid_raw[:].rearrange("p j q -> p q j"))
+        hid_by_col = hid_raw[:].rearrange("p j q -> p q j")
+        nc.vector.tensor_copy(out=hid_bf[:, :CAST_SPLIT, :], in_=hid_by_col[:, :CAST_SPLIT, :])
+        nc.scalar.copy(out=hid_bf[:, CAST_SPLIT:, :], in_=hid_by_col[:, CAST_SPLIT:, :])
+        hid_codes = keep.tile([P, Q], U32, name="hid_codes", align_bytes=64)
+        hid_scales = keep.tile([P, Q], U8, name="hid_scales", align_bytes=64)
+        nc.vector.quantize_mx(
+            out=hid_codes[:].bitcast(FP8X4),
+            scales=hid_scales[:],
+            in_=hid_bf[:].rearrange("p q j -> p (q j)"),
+        )
+
 
         near_t = psum.tile([P, I], F32, name="near_t")
         far_t = psum.tile([P, I], F32, name="far_t")
@@ -100,26 +115,16 @@ def tile_attend_labelforward_kernel(tc, hid, voc_words, voc_scales, old, skip, o
         voc_sc = keep.tile([P, V], U8, name="voc_sc", align_bytes=64)
         nc.vector.tensor_copy(voc_sc[:], store_scales[:].indirect(idx[:]))
 
-        hid_codes = shared.tile([P, Q], U32, name="hid_codes", align_bytes=64, offset=0)
-        hid_scales = keep.tile([P, Q], U8, name="hid_scales", align_bytes=64)
-        nc.vector.quantize_mx(
-            out=hid_codes[:].bitcast(FP8X4),
-            scales=hid_scales[:],
-            in_=hid_bf[:].rearrange("p q j -> p (q j)"),
-        )
-
         last = n_chunks - 1
         neg_a = keep.tile([P, V + 8], F32, name="neg_a")
-        p_un = keep.tile([P, V + 8], F32, name="p_un")
         neg_max = neg_a[:, V:]
         fix = p_un[:, V:]
         sums = keep.tile([P, 8], F32, name="sums")
         terms = keep.tile([P, 8], F32, name="terms")
-        nc.gpsimd.memset(fix[:, last : last + 1], 1.0)
         for c in range(n_chunks):
             n = CHUNKS[c]
             cols = slice(starts[c], starts[c] + n)
-            words = shared.tile([P, n], U32, name="words", align_bytes=64, offset=Q * 4, bufs=2)
+            words = shared.tile([P, n], U32, name="words", align_bytes=64, offset=0, bufs=2)
             nc.vector.tensor_copy(
                 words[:], store_words[:].indirect(idx[:, starts[c] // LANES : (starts[c] + n) // LANES])
             )

@@ -47,15 +47,16 @@ def tile_attend_labelforward_kernel(tc, hid, voc_words, voc_scales, old, skip, o
 
         nc.vector.memset(store_scales[:].bitcast(I32), 0)
         nc.sync.dma_start(idx[:], offs)
-        nc.sync.dma_start(out=hid_raw[:], in_=hid.rearrange("(p j) q -> p j q", j=PACK))
-        with nc.allow_non_contiguous_dma(reason="one value of skip to a partition"):
-            nc.scalar.dma_start(out=skip_col[:], in_=skip[0].rearrange("(j p) -> p j", p=P))
         nc.sync.dma_start(idx2[:], offs2)
+        nc.sync.dma_start(out=hid_raw[:], in_=hid.rearrange("(p j) q -> p j q", j=PACK))
         for r in range(PACK):
             nc.sync.dma_start(
                 out=store_scales[r:P:32, :].bitcast(I32),
                 in_=voc_scales[0, r:16:PACK, :].bitcast(I32),
             )
+        skip_rows = keep.tile([P, P], F32, name="skip_rows")
+        nc.vector.memset(skip_rows[:], 0.0)
+        nc.sync.dma_start(out=skip_rows[: I // P, :], in_=skip[0].rearrange("(j p) -> j p", p=P))
         nc.vector.memset(one[:, :1], 1.0)
         nc.vector.tensor_copy(out=p_un[:, V + n_chunks - 1 : V + n_chunks], in_=one[:, :1])
         nc.vector.memset(ident[:], 0.0)
@@ -82,9 +83,12 @@ def tile_attend_labelforward_kernel(tc, hid, voc_words, voc_scales, old, skip, o
         )
 
 
+        skip_t = psum.tile([P, P], F32, name="skip_t", tag="coef_bank")
+        nc.tensor.transpose(skip_t[:], skip_rows[:], ident[:])
+        nc.scalar.copy(out=skip_col[:], in_=skip_t[:, : I // P])
         near_t = psum.tile([P, I], F32, name="near_t")
         far_t = psum.tile([P, I], F32, name="far_t")
-        coef_ps = psum.tile([P, I], F32, name="coef_ps")
+        coef_ps = psum.tile([P, I], F32, name="coef_ps", tag="coef_bank")
         near_sb = keep.tile([P, I], F32, name="near_sb")
         far_sb = keep.tile([P, I], F32, name="far_sb")
         coef = keep.tile([P, I], F32, name="coef")
@@ -171,9 +175,11 @@ def tile_attend_labelforward_kernel(tc, hid, voc_words, voc_scales, old, skip, o
         nc.vector.reciprocal(out=inv[:], in_=total[:])
         w = keep.tile([P, V], F32, name="w")
         nc.scalar.activation(out=gain[:, :n_chunks], in_=fix[:, :n_chunks], func=ACT.Copy, scale=inv[:])
-        for c in range(n_chunks):
+        for c in (0, 1, 2, 4, 3):
             cols = slice(starts[c], starts[c] + CHUNKS[c])
-            if c < 3:
+            if c == last:
+                nc.scalar.activation(out=w[:, cols], in_=p_un[:, cols], func=ACT.Copy, scale=inv[:])
+            elif c < 3:
                 nc.vector.tensor_scalar(
                     out=w[:, cols], in0=p_un[:, cols], scalar1=fix[:, c : c + 1], scalar2=inv[:],
                     op0=ALU.mult, op1=ALU.mult,

from contextlib import ExitStack

import concourse.mybir as mybir
from concourse.masks import make_identity

D, V, I, Q, T = 512, 2048, 512, 128, 4096
FLOPS = 2 * D * V * Q

F32 = mybir.dt.float32
BF16 = mybir.dt.bfloat16
I32 = mybir.dt.int32
U32 = mybir.dt.uint32
U16 = mybir.dt.uint16
U8 = mybir.dt.uint8
FP8X4 = mybir.dt.float8_e4m3fn_x4
ALU = mybir.AluOpType
ACT = mybir.ActivationFunctionType

P = 128
PACK = 4
LANES = 16
PAD = 8
CHUNKS = (512, 512, 512, 256, 256)
HALF = I // 2
CAST_SPLIT = 80


def tile_attend_labelforward_kernel(tc, hid, voc_words, voc_scales, old, skip, offs, offs2, out):
    nc = tc.nc
    n_chunks = len(CHUNKS)
    starts = [sum(CHUNKS[:c]) for c in range(n_chunks)]

    with ExitStack() as ctx:
        keep = ctx.enter_context(tc.tile_pool(name="keep", bufs=1))
        shared = ctx.enter_context(tc.tile_pool(name="shared", bufs=1))
        late = ctx.enter_context(tc.tile_pool(name="late", bufs=1))
        psum = ctx.enter_context(tc.psum_pool(name="psum", bufs=1))

        idx = keep.tile([P, V // LANES], U16, name="idx")
        idx2 = keep.tile([P, I // LANES], U16, name="idx2")
        store_scales = shared.tile([P, T], U8, name="store_scales", align_bytes=64, offset=0)
        one = late.tile([P, 32], F32, name="one", align_bytes=64, offset=T * 4 - 64)
        p_un = keep.tile([P, V + 8], F32, name="p_un")
        hid_raw = keep.tile([P, PACK, Q], F32, name="hid_raw")
        skip_col = keep.tile([P, I // P], F32, name="skip_col")
        ident = keep.tile([P, P], F32, name="ident")

        nc.vector.memset(store_scales[:].bitcast(I32), 0)
        nc.sync.dma_start(idx[:], offs)
        nc.sync.dma_start(idx2[:], offs2)
        nc.sync.dma_start(out=hid_raw[:], in_=hid.rearrange("(p j) q -> p j q", j=PACK))
        for r in range(PACK):
            nc.sync.dma_start(
                out=store_scales[r:P:32, :].bitcast(I32),
                in_=voc_scales[0, r:16:PACK, :].bitcast(I32),
            )
        skip_rows = keep.tile([P, P], F32, name="skip_rows")
        nc.vector.memset(skip_rows[:], 0.0)
        nc.sync.dma_start(out=skip_rows[: I // P, :], in_=skip[0].rearrange("(j p) -> j p", p=P))
        nc.vector.memset(one[:, :1], 1.0)
        nc.vector.tensor_copy(out=p_un[:, V + n_chunks - 1 : V + n_chunks], in_=one[:, :1])
        nc.vector.memset(ident[:], 0.0)
        make_identity(nc, ident[:], nomemset=True)
        old_pad = late.tile([P, PAD + I], F32, name="old_pad", align_bytes=64, offset=T * 4)
        store_words = late.tile([P, T], U32, name="store_words", align_bytes=64, offset=0)
        nc.sync.dma_start(out=old_pad[:, PAD:], in_=old)
        nc.gpsimd.memset(old_pad[:, PAD - 4 : PAD], 0.0)
        nc.sync.dma_start(
            out=store_words[:].bitcast(I32),
            in_=voc_words[0].rearrange("p n t -> p (n t)").bitcast(I32),
        )

        hid_bf = keep.tile([P, Q, PACK], BF16, name="hid_bf", align_bytes=64)
        hid_by_col = hid_raw[:].rearrange("p j q -> p q j")
        nc.vector.tensor_copy(out=hid_bf[:, :CAST_SPLIT, :], in_=hid_by_col[:, :CAST_SPLIT, :])
        nc.scalar.copy(out=hid_bf[:, CAST_SPLIT:, :], in_=hid_by_col[:, CAST_SPLIT:, :])
        hid_codes = keep.tile([P, Q], U32, name="hid_codes", align_bytes=64)
        hid_scales = keep.tile([P, Q], U8, name="hid_scales", align_bytes=64)
        nc.vector.quantize_mx(
            out=hid_codes[:].bitcast(FP8X4),
            scales=hid_scales[:],
            in_=hid_bf[:].rearrange("p q j -> p (q j)"),
        )


        skip_t = psum.tile([P, P], F32, name="skip_t", tag="coef_bank")
        nc.tensor.transpose(skip_t[:], skip_rows[:], ident[:])
        nc.scalar.copy(out=skip_col[:], in_=skip_t[:, : I // P])
        near_t = psum.tile([P, I], F32, name="near_t")
        far_t = psum.tile([P, I], F32, name="far_t")
        coef_ps = psum.tile([P, I], F32, name="coef_ps", tag="coef_bank")
        near_sb = keep.tile([P, I], F32, name="near_sb")
        far_sb = keep.tile([P, I], F32, name="far_sb")
        coef = keep.tile([P, I], F32, name="coef")
        for j in range(I // P):
            cols = slice(j * P, (j + 1) * P)
            for back in (0, 1):
                first = PAD + j * P - back
                nc.tensor.matmul(
                    near_t[:, cols], lhsT=old_pad[:, first : first + P], rhs=ident[:],
                    is_transpose=True, start=(back == 0), stop=(back == 1),
                )
        for j in range(I // P):
            first = PAD + j * P - 2
            nc.tensor.transpose(far_t[:, j * P : (j + 1) * P], old_pad[:, first : first + P], ident[:])
        nc.scalar.copy(out=near_sb[:], in_=near_t[:])
        for j in range(I // P):
            cols = slice(j * P, (j + 1) * P)
            nc.scalar.activation(out=far_sb[:, cols], in_=far_t[:, cols], func=ACT.Copy, scale=skip_col[:, j : j + 1])
        for j in range(I // P):
            cols = slice(j * P, (j + 1) * P)
            for k, part in enumerate((near_sb, far_sb)):
                nc.tensor.matmul(
                    coef_ps[:, cols], lhsT=part[:, cols], rhs=ident[:],
                    is_transpose=True, start=(k == 0), stop=(k == 1),
                )
        nc.scalar.copy(out=coef[:], in_=coef_ps[:])

        voc_sc = keep.tile([P, V], U8, name="voc_sc", align_bytes=64)
        nc.vector.tensor_copy(voc_sc[:], store_scales[:].indirect(idx[:]))

        last = n_chunks - 1
        neg_a = keep.tile([P, V + 8], F32, name="neg_a")
        neg_max = neg_a[:, V:]
        fix = p_un[:, V:]
        sums = keep.tile([P, 8], F32, name="sums")
        terms = keep.tile([P, 8], F32, name="terms")
        for c in range(n_chunks):
            n = CHUNKS[c]
            cols = slice(starts[c], starts[c] + n)
            words = shared.tile([P, n], U32, name="words", align_bytes=64, offset=0, bufs=2)
            nc.vector.tensor_copy(
                words[:], store_words[:].indirect(idx[:, starts[c] // LANES : (starts[c] + n) // LANES])
            )
            scores = psum.tile([P, n], F32, name="scores%d" % c)
            nc.tensor.matmul_mx(
                out=scores[:],
                lhsT=hid_codes[:].bitcast(FP8X4),
                lhsT_scale=hid_scales[:],
                rhs=words[:].bitcast(FP8X4),
                rhs_scale=voc_sc[:, cols],
                start=True,
                stop=True,
            )
            nc.vector.tensor_scalar(
                out=neg_a[:, cols],
                in0=scores[:],
                scalar1=-1.0,
                scalar2=(neg_max[:, c - 1 : c] if c > 0 else None),
                op0=ALU.mult,
                op1=ALU.min,
                accum_out=neg_max[:, c : c + 1],
            )
            if c < last:
                nc.scalar.activation(
                    out=p_un[:, cols], in_=neg_a[:, cols], func=ACT.Exp,
                    scale=-1.0, bias=neg_max[:, c : c + 1], accum_out=sums[:, c : c + 1],
                )
        nc.vector.tensor_scalar(
            out=terms[:, :last], in0=sums[:, :last], scalar1=-1.0, scalar2=None, op0=ALU.add
        )
        nc.scalar.activation(
            out=p_un[:, starts[last] : V + last], in_=neg_a[:, starts[last] : V + last], func=ACT.Exp,
            scale=-1.0, bias=neg_max[:, last : last + 1], accum_out=terms[:, last : last + 1],
        )

        parts = keep.tile([P, 8], F32, name="parts")
        total = keep.tile([P, 1], F32, name="total")
        inv = keep.tile([P, 1], F32, name="inv")
        gain = keep.tile([P, 8], F32, name="gain")
        nc.vector.scalar_tensor_tensor(
            out=parts[:, :n_chunks], in0=terms[:, :n_chunks], scalar=1.0 / V, in1=fix[:, :n_chunks],
            op0=ALU.mult, op1=ALU.mult, accum_out=total[:],
        )
        nc.vector.reciprocal(out=inv[:], in_=total[:])
        w = keep.tile([P, V], F32, name="w")
        nc.scalar.activation(out=gain[:, :n_chunks], in_=fix[:, :n_chunks], func=ACT.Copy, scale=inv[:])
        for c in (0, 1, 2, 4, 3):
            cols = slice(starts[c], starts[c] + CHUNKS[c])
            if c == last:
                nc.scalar.activation(out=w[:, cols], in_=p_un[:, cols], func=ACT.Copy, scale=inv[:])
            elif c < 3:
                nc.vector.tensor_scalar(
                    out=w[:, cols], in0=p_un[:, cols], scalar1=fix[:, c : c + 1], scalar2=inv[:],
                    op0=ALU.mult, op1=ALU.mult,
                )
            else:
                nc.scalar.activation(out=w[:, cols], in_=p_un[:, cols], func=ACT.Copy, scale=gain[:, c : c + 1])

        res_a = keep.tile([P, HALF], F32, name="res_a")
        picked = keep.tile([P, HALF], F32, name="picked")
        res_b = keep.tile([P, HALF], F32, name="res_b")
        nc.vector.tensor_tensor(res_a[:], w[:].indirect(idx2[:, : HALF // LANES]), coef[:, :HALF], ALU.mult)
        nc.scalar.activation(picked[:], w[:].indirect(idx2[:, HALF // LANES :]), ACT.Copy)
        nc.sync.dma_start(out=out[:, :HALF], in_=res_a[:])
        nc.vector.tensor_tensor(res_b[:], picked[:], coef[:, HALF:], ALU.mult)
        nc.sync.dma_start(out=out[:, HALF:], in_=res_b[:])
